import numpy as np
import ml_dtypes


def mxq(x, axis, fmt="e4m3"):
    dtype, down = {"e4m3": (ml_dtypes.float8_e4m3fn, 7), "e5m2": (ml_dtypes.float8_e5m2, 14)}[fmt]
    v = np.moveaxis(np.asarray(x, np.float32).astype(ml_dtypes.bfloat16).astype(np.float64), axis, -1)
    blocks = v.reshape(v.shape[:-1] + (-1, 32))
    amax = np.abs(blocks).max(-1, keepdims=True)
    byte = np.maximum(np.where(amax > 0, np.frexp(amax)[1] - 1 + 127, 0) - down, 1)
    scale = np.exp2(byte - 127.0)
    codes = (blocks / scale).astype(np.float32).astype(dtype).astype(np.float64)
    return np.moveaxis((codes * scale).reshape(v.shape), -1, axis)


WIDE = False


def mx_kscale(k):
    if not WIDE:
        return np.ones(k)
    levels = np.array([10, -10, 5, -5, 0])
    if k % 512:
        return np.exp2(np.random.permutation(np.resize(levels, k // 32))).repeat(32)
    a = np.empty((k // 512, 16))
    for p in range(k // 512):
        a[p, :8] = np.random.permutation(np.resize(levels, 8))
        for g in range(8):
            far = levels[np.abs(levels - a[p, g]) >= 10]
            a[p, g + 8] = far[np.random.randint(len(far))]
    return np.exp2(a.ravel()).repeat(32)


def f64(x):
    return np.asarray(x).astype(np.float64)


def striped(idx):
    return np.tile(idx.reshape(-1, 16).T, (8, 1)).astype(np.uint16)


def unstriped(offs):
    return offs[:16].T.reshape(-1).astype(np.int64)


def striped8(idx):
    return np.concatenate([x.reshape(-1, 16).T for x in idx]).astype(np.uint16)


def runs(offs, k):
    lists = np.stack([offs[16 * r : 16 * r + 16].T.reshape(-1) for r in range(8)]).astype(np.int64)
    return lists[np.arange(k) % 512 // 64]


def pack_weight(w):
    k, n = w.shape
    w = f64(np.asarray(w, np.float32).astype(ml_dtypes.bfloat16)).reshape(k // 32, 32, n)
    amax = np.abs(w).max(1)
    byte = np.clip(np.where(amax > 0, np.frexp(amax)[1] - 1 + 127 - 7, 1), 1, 254)
    scaled = (w * np.exp2(127.0 - byte)[:, None, :]).reshape(k, n).astype(np.float32)
    words = np.ascontiguousarray(scaled.reshape(k // 512, 128, 4, n).transpose(0, 1, 3, 2)).astype(ml_dtypes.float8_e4m3fn).view(np.uint8)
    return words, np.ascontiguousarray(byte.astype(np.uint8).reshape(k // 512, 16, n))


def unpack_weight(words, scales):
    g, p, n, _ = words.shape
    vals = np.ascontiguousarray(words).view(ml_dtypes.float8_e4m3fn).astype(np.float64) * np.repeat(np.exp2(scales.astype(np.float64) - 127.0), 8, axis=1)[..., None]
    return vals.transpose(0, 1, 3, 2).reshape(g * 512, n)


K, T, S, N, H, U = 512, 2048, 512, 512, 512, 1024


def setup_inputs():
    n = np.random.standard_normal
    s = mx_kscale(K)[:, None]
    u = mx_kscale(H)
    packed_xT = pack_weight(n((K, T)) * s)
    return {
        "x_words": packed_xT[0],
        "x_scales": packed_xT[1],
        "w1": (n((K, H)) / np.sqrt(K) / s).astype(np.float32),
        "gn": (np.random.uniform(0.5, 1.5, (H, 1)) * u[:, None]).astype(np.float32),
        "w2": (n((H, N)) / np.sqrt(H) / u[:, None]).astype(np.float32),
        "mem": n((N, U)).astype(np.float32),
        "offs": striped(np.random.permutation(T)[:S]),
        "p1": striped8(np.stack([np.random.permutation(S) for _ in range(8)])),
        "p2": striped8(np.stack([np.random.permutation(S) for _ in range(8)])),
        "p3": striped8(np.stack([np.random.permutation(S) for _ in range(8)])),
        "p4": striped8(np.stack([np.random.permutation(S) for _ in range(8)])),
        "slot": striped8(np.stack([np.random.permutation(U)[:S] for _ in range(8)])),
    }


def reference(x_words, x_scales, w1, gn, w2, mem, offs, p1, p2, p3, p4, slot):
    xq = unpack_weight(x_words, x_scales)[:, unstriped(offs)]
    y = mxq(f64(w1), 0, "e4m3").T @ xq
    a = y[np.arange(H)[:, None], runs(p1, H)]
    b = y[np.arange(H)[:, None], runs(p2, H)]
    m1 = np.maximum(np.minimum(y, a), np.minimum(np.maximum(y, a), b))
    c = m1[np.arange(H)[:, None], runs(p3, H)]
    d = m1[np.arange(H)[:, None], runs(p4, H)]
    z = f64(gn) * (0.5 * y - (np.maximum(np.minimum(m1, c), np.minimum(np.maximum(m1, c), d))))
    h = mxq(f64(w2), 0, "e4m3").T @ mxq(z, 0, "e4m3")
    out = f64(mem).copy()
    out[np.arange(N)[:, None], runs(slot, N)] = h
    return out

@@ -1,0 +1,200 @@
+from contextlib import ExitStack
+
+import concourse.mybir as mybir
+from concourse.masks import make_identity
+
+K, T, S, N, H, U = 512, 2048, 512, 512, 512, 1024
+FLOPS = 2 * K * H * S + 2 * H * N * S
+
+F32 = mybir.dt.float32
+BF16 = mybir.dt.bfloat16
+I32 = mybir.dt.int32
+U32 = mybir.dt.uint32
+U16 = mybir.dt.uint16
+U8 = mybir.dt.uint8
+FP8X4 = mybir.dt.float8_e4m3fn_x4
+ALU = mybir.AluOpType
+COPY = mybir.ActivationFunctionType.Copy
+
+P = 128
+PACK = 4
+HALVES = 2
+HALF = S // HALVES
+CHUNKS = HALF // P
+LIST_COLS = S // 16
+
+
+def tile_picked_medfilt2_none_p_kernel(
+    tc, x_words, x_scales, w1, gn, w2, mem, offs, p1, p2, p3, p4, slot, out
+):
+    nc = tc.nc
+    with ExitStack() as ctx:
+        lists = ctx.enter_context(tc.tile_pool(name="lists", bufs=1))
+        keep = ctx.enter_context(tc.tile_pool(name="keep", bufs=1))
+        work = ctx.enter_context(tc.tile_pool(name="work", bufs=2))
+        psum = ctx.enter_context(tc.psum_pool(name="psum", bufs=1))
+
+        def load_list(src, name):
+            tile = lists.tile([P, LIST_COLS], U16, name=name)
+            nc.sync.dma_start(tile[:], src)
+            return tile
+
+        def add_transposed(dst, terms):
+            for i, term in enumerate(terms):
+                nc.tensor.matmul(dst, lhsT=term, rhs=ident[:], is_transpose=True, start=(i == 0), stop=(i == len(terms) - 1))
+
+        def minmod(u, v, dst, width):
+            upper = work.tile([P, width], F32, name="upper%d" % width)
+            nc.vector.scalar_tensor_tensor(upper[:], u[:], 0.0, v[:], ALU.max, ALU.min)
+            nc.vector.scalar_tensor_tensor(dst, u[:], 0.0, upper[:], ALU.min, ALU.max)
+
+        x_scale_table = keep.tile([P, T], U8, name="x_scale_table")
+        nc.vector.memset(x_scale_table[:].bitcast(I32), 0)
+        offs_t = load_list(offs, "offs_t")
+        for q in range(4):
+            nc.scalar.dma_start(x_scale_table[32 * q : 32 * q + 4, :].bitcast(I32), x_scales[0, 4 * q : 4 * q + 4, :].bitcast(I32))
+        w1_raw = keep.tile([P, PACK, H], F32, name="w1_raw")
+        nc.sync.dma_start(w1_raw[:], w1.rearrange("(p j) c -> p j c", j=PACK))
+        x_word_table = keep.tile([P, T], U32, name="x_word_table")
+        nc.sync.dma_start(x_word_table[:].bitcast(I32), x_words[0].rearrange("p c r -> p (c r)").bitcast(I32))
+        gain = keep.tile([P, PACK], F32, name="gain")
+        nc.sync.dma_start(gain[:], gn.rearrange("(p t) o -> p (t o)", t=PACK))
+        p1_t = load_list(p1, "p1_t")
+        p2_t = load_list(p2, "p2_t")
+        p3_t = load_list(p3, "p3_t")
+        p4_t = load_list(p4, "p4_t")
+        slot_t = load_list(slot, "slot_t")
+        w2_raw = keep.tile([P, PACK, N], F32, name="w2_raw")
+        nc.sync.dma_start(w2_raw[:], w2.rearrange("(p j) c -> p j c", j=PACK))
+        pages = []
+        for t in range(PACK):
+            page = keep.tile([P, U], F32, name="page%d" % t)
+            nc.sync.dma_start(page[:], mem.rearrange("(p t) u -> t p u", t=PACK)[t])
+            pages.append(page)
+
+        ident = keep.tile([P, P], F32, name="ident")
+        make_identity(nc, ident[:])
+        y_windows = []
+        for t in range(PACK):
+            window = keep.tile([P, 2 * S], F32, name="y_window%d" % t)
+            nc.gpsimd.memset(window[:, S:], 0.0)
+            y_windows.append(window)
+
+        x_scale = keep.tile([P, S], U8, name="x_scale", align_bytes=64)
+        nc.vector.tensor_copy(x_scale[:], x_scale_table[:].indirect(offs_t[:]))
+        w1_dealt = w1_raw[:].rearrange("p j (m t) -> p t m j", t=PACK)
+        w1_grouped = []
+        for t in range(PACK):
+            grouped = keep.tile([P, P, PACK], BF16, name="w1_grouped%d" % t, align_bytes=64)
+            if t < 2:
+                nc.vector.tensor_copy(grouped[:], w1_dealt[:, t])
+            else:
+                nc.scalar.copy(grouped[:], w1_dealt[:, t])
+            w1_grouped.append(grouped)
+
+        def quantise_w1(t):
+            codes = keep.tile([P, P], U32, name="w1_codes%d" % t, align_bytes=64)
+            scales = keep.tile([P, P], U8, name="w1_scales%d" % t, align_bytes=64)
+            nc.vector.quantize_mx(out=codes[:].bitcast(FP8X4), scales=scales[:], in_=w1_grouped[t][:].rearrange("p m j -> p (m j)"))
+            return codes, scales
+
+        w1_mx = [quantise_w1(0)]
+        x_code = keep.tile([P, S], U32, name="x_code", align_bytes=64)
+        for h in range(HALVES):
+            nc.vector.tensor_copy(x_code[:, h * HALF : (h + 1) * HALF], x_word_table[:].indirect(offs_t[:, h * HALF // 16 : (h + 1) * HALF // 16]))
+        w1_mx.extend(quantise_w1(t) for t in range(1, PACK))
+
+        half_y, r1, m1_windows, m1_plain = [], [], [], []
+        y_plain = []
+        for t in range(PACK):
+            codes, scales = w1_mx[t]
+            plain = keep.tile([P, S], F32, name="y_plain%d" % t)
+            width = HALF if t == 0 else S
+            for s0 in range(0, S, width):
+                cols = slice(s0, s0 + width)
+                acc = psum.tile([P, S], F32, name="acc", bufs=2)
+                nc.tensor.matmul_mx(out=acc[:, :width], lhsT=codes[:].bitcast(FP8X4), lhsT_scale=scales[:], rhs=x_code[:, cols].bitcast(FP8X4), rhs_scale=x_scale[:, cols], start=True, stop=True)
+                nc.scalar.activation(y_windows[t][:, cols], acc[:, :width], COPY, scale=gain[:, t : t + 1])
+                nc.scalar.activation(plain[:, cols], acc[:, :width], COPY, scale=gain[:, t : t + 1])
+            y_plain.append(plain)
+
+        for t in range(PACK):
+            u = work.tile([P, S], F32, name="u1")
+            nc.vector.tensor_tensor(u[:], y_windows[t][:].indirect(p1_t[:]), y_plain[t][:], ALU.subtract)
+            v = work.tile([P, S], F32, name="v1")
+            nc.vector.tensor_tensor(v[:], y_windows[t][:].indirect(p2_t[:]), y_plain[t][:], ALU.subtract)
+            step = keep.tile([P, S], F32, name="r1_%d" % t)
+            minmod(u, v, step[:], S)
+            r1.append(step)
+            turned = psum.tile([P, S // P, P], F32, name="turned", bufs=2)
+            for c in range(S // P):
+                cols = slice(c * P, (c + 1) * P)
+                add_transposed(turned[:, c, :], [y_plain[t][:, cols], step[:, cols]])
+            turned_sb = work.tile([P, S // P, P], F32, name="turned_sb")
+            nc.scalar.copy(turned_sb[:], turned[:])
+            back = psum.tile([P, S // P, P], F32, name="back", bufs=1)
+            for c in range(S // P):
+                add_transposed(back[:, c, :], [turned_sb[:, c, :]])
+            window = keep.tile([P, S], F32, name="m1_window%d" % t)
+            nc.scalar.copy(window[:], back[:].rearrange("p c s -> p (c s)"))
+            plain = keep.tile([P, S], F32, name="m1_plain%d" % t)
+            nc.scalar.copy(plain[:], back[:].rearrange("p c s -> p (c s)"))
+            m1_windows.append(window)
+            m1_plain.append(plain)
+
+        for t in range(PACK):
+            half = keep.tile([P, S], F32, name="half_y%d" % t)
+            nc.scalar.activation(half[:], y_plain[t][:], COPY, scale=0.5)
+            half_y.append(half)
+
+        w2_grouped = keep.tile([P, PACK, P, PACK], BF16, name="w2_grouped", align_bytes=64)
+        for t in range(PACK):
+            nc.scalar.copy(w2_grouped[:, t], w2_raw[:].rearrange("p j (m t) -> p t m j", t=PACK)[:, t])
+        w2_codes = keep.tile([P, N], U32, name="w2_codes", align_bytes=64)
+        w2_scales = keep.tile([P, N], U8, name="w2_scales", align_bytes=64)
+        nc.vector.quantize_mx(out=w2_codes[:].bitcast(FP8X4), scales=w2_scales[:], in_=w2_grouped[:].rearrange("p t m j -> p (t m j)"))
+
+        z_grouped = []
+        for h in range(HALVES):
+            entries = slice(h * HALF // 16, (h + 1) * HALF // 16)
+            samples = slice(h * HALF, (h + 1) * HALF)
+            z_turned = [psum.tile([P, PACK, P], F32, name="z_turned%d" % c, bufs=1) for c in range(CHUNKS)]
+            for t in range(PACK):
+                u = work.tile([P, HALF], F32, name="u2")
+                nc.vector.tensor_tensor(u[:], m1_windows[t][:].indirect(p3_t[:, entries]), m1_plain[t][:, samples], ALU.subtract)
+                v = work.tile([P, HALF], F32, name="v2")
+                nc.vector.tensor_tensor(v[:], m1_windows[t][:].indirect(p4_t[:, entries]), m1_plain[t][:, samples], ALU.subtract)
+                r2 = work.tile([P, HALF], F32, name="r2")
+                minmod(u, v, r2[:], HALF)
+                for c in range(CHUNKS):
+                    cols = slice(h * HALF + c * P, h * HALF + (c + 1) * P)
+                    add_transposed(z_turned[c][:, t, :], [half_y[t][:, cols], r1[t][:, cols], r2[:, c * P : (c + 1) * P]])
+            pairs = psum.tile([P, CHUNKS, 2, P], F32, name="pairs", bufs=1)
+            for c in range(CHUNKS):
+                z_rows = work.tile([P, 2, P, 2], BF16, name="z_rows")
+                nc.scalar.activation(z_rows[:], z_turned[c][:].rearrange("s (u e) p -> s u p e", e=2), COPY, scale=-1.0)
+                words = z_rows[:].rearrange("s u p e -> s (u p e)").bitcast(F32)
+                for w in range(2):
+                    nc.tensor.transpose(pairs[:, c, w, :], words[:, w * P : (w + 1) * P], ident[:])
+            grouped = work.tile([P, HALF * PACK], BF16, name="z_grouped", align_bytes=64)
+            nc.scalar.copy(
+                grouped[:].bitcast(F32).rearrange("p (c s w) -> p c s w", c=CHUNKS, w=2),
+                pairs[:].rearrange("p c w s -> p c s w"),
+            )
+            z_grouped.append(grouped)
+
+        for h in range(HALVES):
+            entries = slice(h * HALF // 16, (h + 1) * HALF // 16)
+            z_codes = work.tile([P, HALF], U32, name="z_codes", align_bytes=64)
+            z_scales = work.tile([P, HALF], U8, name="z_scales", align_bytes=64)
+            nc.vector.quantize_mx(out=z_codes[:].bitcast(FP8X4), scales=z_scales[:], in_=z_grouped[h][:])
+            for t in range(PACK):
+                cols = slice(t * P, (t + 1) * P)
+                acc = psum.tile([P, S], F32, name="acc", bufs=2)
+                nc.tensor.matmul_mx(out=acc[:, :HALF], lhsT=w2_codes[:, cols].bitcast(FP8X4), lhsT_scale=w2_scales[:, cols], rhs=z_codes[:].bitcast(FP8X4), rhs_scale=z_scales[:], start=True, stop=True)
+                result = work.tile([P, HALF], F32, name="result", bufs=4)
+                nc.scalar.copy(result[:], acc[:, :HALF])
+                nc.vector.tensor_copy(pages[t][:].indirect(slot_t[:, entries]), result[:])
+
+        for t in range(PACK):
+            nc.sync.dma_start(out.rearrange("(p t) u -> t p u", t=PACK)[t], pages[t][:])

@@ -51,14 +51,15 @@ def tile_picked_medfilt2_none_p_kernel(
         x_scale_table = keep.tile([P, T], U8, name="x_scale_table")
         nc.vector.memset(x_scale_table[:].bitcast(I32), 0)
         offs_t = load_list(offs, "offs_t")
+        x_scale_rows = keep.tile([P, T // 4], I32, name="x_scale_rows")
         for q in range(4):
-            nc.scalar.dma_start(x_scale_table[32 * q : 32 * q + 4, :].bitcast(I32), x_scales[0, 4 * q : 4 * q + 4, :].bitcast(I32))
+            nc.sync.dma_start(x_scale_rows[32 * q : 32 * q + 4, :], x_scales[0, 4 * q : 4 * q + 4, :].bitcast(I32))
         w1_raw = keep.tile([P, PACK, H], F32, name="w1_raw")
         nc.sync.dma_start(w1_raw[:], w1.rearrange("(p j) c -> p j c", j=PACK))
         x_word_table = keep.tile([P, T], U32, name="x_word_table")
         nc.sync.dma_start(x_word_table[:].bitcast(I32), x_words[0].rearrange("p c r -> p (c r)").bitcast(I32))
         gain = keep.tile([P, PACK], F32, name="gain")
-        nc.sync.dma_start(gain[:], gn.rearrange("(p t) o -> p (t o)", t=PACK))
+        nc.scalar.dma_start(gain[:], gn.rearrange("(p t) o -> p (t o)", t=PACK))
         p1_t = load_list(p1, "p1_t")
         p2_t = load_list(p2, "p2_t")
         p3_t = load_list(p3, "p3_t")
@@ -80,6 +81,8 @@ def tile_picked_medfilt2_none_p_kernel(
             nc.gpsimd.memset(window[:, S:], 0.0)
             y_windows.append(window)
 
+        for q in range(4):
+            nc.vector.tensor_copy(x_scale_table[32 * q : 32 * q + 4, :].bitcast(I32), x_scale_rows[32 * q : 32 * q + 4, :])
         x_scale = keep.tile([P, S], U8, name="x_scale", align_bytes=64)
         nc.vector.tensor_copy(x_scale[:], x_scale_table[:].indirect(offs_t[:]))
         w1_dealt = w1_raw[:].rearrange("p j (m t) -> p t m j", t=PACK)
@@ -115,12 +118,18 @@ def tile_picked_medfilt2_none_p_kernel(
                 acc = psum.tile([P, S], F32, name="acc", bufs=2)
                 nc.tensor.matmul_mx(out=acc[:, :width], lhsT=codes[:].bitcast(FP8X4), lhsT_scale=scales[:], rhs=x_code[:, cols].bitcast(FP8X4), rhs_scale=x_scale[:, cols], start=True, stop=True)
                 nc.scalar.activation(y_windows[t][:, cols], acc[:, :width], COPY, scale=gain[:, t : t + 1])
-                nc.scalar.activation(plain[:, cols], acc[:, :width], COPY, scale=gain[:, t : t + 1])
+                if (t, s0) == (0, 0):
+                    nc.vector.tensor_scalar(plain[:, cols], acc[:, :width], gain[:, t : t + 1], None, ALU.mult)
+                else:
+                    nc.scalar.activation(plain[:, cols], acc[:, :width], COPY, scale=gain[:, t : t + 1])
             y_plain.append(plain)
 
         for t in range(PACK):
             u = work.tile([P, S], F32, name="u1")
-            nc.vector.tensor_tensor(u[:], y_windows[t][:].indirect(p1_t[:]), y_plain[t][:], ALU.subtract)
+            width = HALF if t == 0 else S
+            for s0 in range(0, S, width):
+                cols = slice(s0, s0 + width)
+                nc.vector.tensor_tensor(u[:, cols], y_windows[t][:].indirect(p1_t[:, s0 // 16 : (s0 + width) // 16]), y_plain[t][:, cols], ALU.subtract)
             v = work.tile([P, S], F32, name="v1")
             nc.vector.tensor_tensor(v[:], y_windows[t][:].indirect(p2_t[:]), y_plain[t][:], ALU.subtract)
             step = keep.tile([P, S], F32, name="r1_%d" % t)
@@ -154,21 +163,25 @@ def tile_picked_medfilt2_none_p_kernel(
         w2_scales = keep.tile([P, N], U8, name="w2_scales", align_bytes=64)
         nc.vector.quantize_mx(out=w2_codes[:].bitcast(FP8X4), scales=w2_scales[:], in_=w2_grouped[:].rearrange("p t m j -> p (t m j)"))
 
-        z_grouped = []
+        z_mx = []
         for h in range(HALVES):
             entries = slice(h * HALF // 16, (h + 1) * HALF // 16)
             samples = slice(h * HALF, (h + 1) * HALF)
             z_turned = [psum.tile([P, PACK, P], F32, name="z_turned%d" % c, bufs=1) for c in range(CHUNKS)]
-            for t in range(PACK):
-                u = work.tile([P, HALF], F32, name="u2")
-                nc.vector.tensor_tensor(u[:], m1_windows[t][:].indirect(p3_t[:, entries]), m1_plain[t][:, samples], ALU.subtract)
-                v = work.tile([P, HALF], F32, name="v2")
-                nc.vector.tensor_tensor(v[:], m1_windows[t][:].indirect(p4_t[:, entries]), m1_plain[t][:, samples], ALU.subtract)
-                r2 = work.tile([P, HALF], F32, name="r2")
-                minmod(u, v, r2[:], HALF)
-                for c in range(CHUNKS):
-                    cols = slice(h * HALF + c * P, h * HALF + (c + 1) * P)
-                    add_transposed(z_turned[c][:, t, :], [half_y[t][:, cols], r1[t][:, cols], r2[:, c * P : (c + 1) * P]])
+            for t0 in range(0, PACK, 2):
+                u = work.tile([P, 2 * HALF], F32, name="u2")
+                v = work.tile([P, 2 * HALF], F32, name="v2")
+                for i in range(2):
+                    part = slice(i * HALF, (i + 1) * HALF)
+                    nc.vector.tensor_tensor(u[:, part], m1_windows[t0 + i][:].indirect(p3_t[:, entries]), m1_plain[t0 + i][:, samples], ALU.subtract)
+                    nc.vector.tensor_tensor(v[:, part], m1_windows[t0 + i][:].indirect(p4_t[:, entries]), m1_plain[t0 + i][:, samples], ALU.subtract)
+                r2 = work.tile([P, 2 * HALF], F32, name="r2")
+                minmod(u, v, r2[:], 2 * HALF)
+                for i in range(2):
+                    t = t0 + i
+                    for c in range(CHUNKS):
+                        cols = slice(h * HALF + c * P, h * HALF + (c + 1) * P)
+                        add_transposed(z_turned[c][:, t, :], [half_y[t][:, cols], r1[t][:, cols], r2[:, i * HALF + c * P : i * HALF + (c + 1) * P]])
             pairs = psum.tile([P, CHUNKS, 2, P], F32, name="pairs", bufs=1)
             for c in range(CHUNKS):
                 z_rows = work.tile([P, 2, P, 2], BF16, name="z_rows")
@@ -181,20 +194,25 @@ def tile_picked_medfilt2_none_p_kernel(
                 grouped[:].bitcast(F32).rearrange("p (c s w) -> p c s w", c=CHUNKS, w=2),
                 pairs[:].rearrange("p c w s -> p c s w"),
             )
-            z_grouped.append(grouped)
-
-        for h in range(HALVES):
-            entries = slice(h * HALF // 16, (h + 1) * HALF // 16)
             z_codes = work.tile([P, HALF], U32, name="z_codes", align_bytes=64)
             z_scales = work.tile([P, HALF], U8, name="z_scales", align_bytes=64)
-            nc.vector.quantize_mx(out=z_codes[:].bitcast(FP8X4), scales=z_scales[:], in_=z_grouped[h][:])
+            nc.vector.quantize_mx(out=z_codes[:].bitcast(FP8X4), scales=z_scales[:], in_=grouped[:])
+            z_mx.append((z_codes, z_scales))
+
+        def put_back(h, t, acc):
+            z_codes, z_scales = z_mx[h]
+            cols = slice(t * P, (t + 1) * P)
+            nc.tensor.matmul_mx(out=acc[:, :HALF], lhsT=w2_codes[:, cols].bitcast(FP8X4), lhsT_scale=w2_scales[:, cols], rhs=z_codes[:].bitcast(FP8X4), rhs_scale=z_scales[:], start=True, stop=True)
+            result = work.tile([P, HALF], F32, name="result", bufs=4)
+            nc.scalar.copy(result[:], acc[:, :HALF])
+            nc.vector.tensor_copy(pages[t][:].indirect(slot_t[:, h * HALF // 16 : (h + 1) * HALF // 16]), result[:])
+
+        for h in range(HALVES):
             for t in range(PACK):
-                cols = slice(t * P, (t + 1) * P)
-                acc = psum.tile([P, S], F32, name="acc", bufs=2)
-                nc.tensor.matmul_mx(out=acc[:, :HALF], lhsT=w2_codes[:, cols].bitcast(FP8X4), lhsT_scale=w2_scales[:, cols], rhs=z_codes[:].bitcast(FP8X4), rhs_scale=z_scales[:], start=True, stop=True)
-                result = work.tile([P, HALF], F32, name="result", bufs=4)
-                nc.scalar.copy(result[:], acc[:, :HALF])
-                nc.vector.tensor_copy(pages[t][:].indirect(slot_t[:, entries]), result[:])
+                if (h, t) == (0, PACK - 1):
+                    put_back(h, t, psum.tile([P, S], F32, name="pairs", bufs=1))
+                else:
+                    put_back(h, t, psum.tile([P, S], F32, name="acc", bufs=2))
 
         for t in range(PACK):
             nc.sync.dma_start(out.rearrange("(p t) u -> t p u", t=PACK)[t], pages[t][:])

from contextlib import ExitStack

import concourse.mybir as mybir
from concourse.masks import make_identity

K, T, S, N, H, U = 512, 2048, 512, 512, 512, 1024
FLOPS = 2 * K * H * S + 2 * H * N * S

F32 = mybir.dt.float32
BF16 = mybir.dt.bfloat16
I32 = mybir.dt.int32
U32 = mybir.dt.uint32
U16 = mybir.dt.uint16
U8 = mybir.dt.uint8
FP8X4 = mybir.dt.float8_e4m3fn_x4
ALU = mybir.AluOpType
COPY = mybir.ActivationFunctionType.Copy

P = 128
PACK = 4
HALVES = 2
HALF = S // HALVES
CHUNKS = HALF // P
LIST_COLS = S // 16


def tile_picked_medfilt2_none_p_kernel(
    tc, x_words, x_scales, w1, gn, w2, mem, offs, p1, p2, p3, p4, slot, out
):
    nc = tc.nc
    with ExitStack() as ctx:
        lists = ctx.enter_context(tc.tile_pool(name="lists", bufs=1))
        keep = ctx.enter_context(tc.tile_pool(name="keep", bufs=1))
        work = ctx.enter_context(tc.tile_pool(name="work", bufs=2))
        psum = ctx.enter_context(tc.psum_pool(name="psum", bufs=1))

        def load_list(src, name):
            tile = lists.tile([P, LIST_COLS], U16, name=name)
            nc.sync.dma_start(tile[:], src)
            return tile

        def add_transposed(dst, terms):
            for i, term in enumerate(terms):
                nc.tensor.matmul(dst, lhsT=term, rhs=ident[:], is_transpose=True, start=(i == 0), stop=(i == len(terms) - 1))

        def minmod(u, v, dst, width):
            upper = work.tile([P, width], F32, name="upper%d" % width)
            nc.vector.scalar_tensor_tensor(upper[:], u[:], 0.0, v[:], ALU.max, ALU.min)
            nc.vector.scalar_tensor_tensor(dst, u[:], 0.0, upper[:], ALU.min, ALU.max)

        x_scale_table = keep.tile([P, T], U8, name="x_scale_table")
        nc.vector.memset(x_scale_table[:].bitcast(I32), 0)
        offs_t = load_list(offs, "offs_t")
        x_scale_rows = keep.tile([P, T // 4], I32, name="x_scale_rows")
        for q in range(4):
            nc.sync.dma_start(x_scale_rows[32 * q : 32 * q + 4, :], x_scales[0, 4 * q : 4 * q + 4, :].bitcast(I32))
        w1_raw = keep.tile([P, PACK, H], F32, name="w1_raw")
        nc.sync.dma_start(w1_raw[:], w1.rearrange("(p j) c -> p j c", j=PACK))
        x_word_table = keep.tile([P, T], U32, name="x_word_table")
        nc.sync.dma_start(x_word_table[:].bitcast(I32), x_words[0].rearrange("p c r -> p (c r)").bitcast(I32))
        gain = keep.tile([P, PACK], F32, name="gain")
        nc.scalar.dma_start(gain[:], gn.rearrange("(p t) o -> p (t o)", t=PACK))
        p1_t = load_list(p1, "p1_t")
        p2_t = load_list(p2, "p2_t")
        p3_t = load_list(p3, "p3_t")
        p4_t = load_list(p4, "p4_t")
        slot_t = load_list(slot, "slot_t")
        w2_raw = keep.tile([P, PACK, N], F32, name="w2_raw")
        nc.sync.dma_start(w2_raw[:], w2.rearrange("(p j) c -> p j c", j=PACK))
        pages = []
        for t in range(PACK):
            page = keep.tile([P, U], F32, name="page%d" % t)
            nc.sync.dma_start(page[:], mem.rearrange("(p t) u -> t p u", t=PACK)[t])
            pages.append(page)

        ident = keep.tile([P, P], F32, name="ident")
        make_identity(nc, ident[:])
        y_windows = []
        for t in range(PACK):
            window = keep.tile([P, 2 * S], F32, name="y_window%d" % t)
            nc.gpsimd.memset(window[:, S:], 0.0)
            y_windows.append(window)

        for q in range(4):
            nc.vector.tensor_copy(x_scale_table[32 * q : 32 * q + 4, :].bitcast(I32), x_scale_rows[32 * q : 32 * q + 4, :])
        x_scale = keep.tile([P, S], U8, name="x_scale", align_bytes=64)
        nc.vector.tensor_copy(x_scale[:], x_scale_table[:].indirect(offs_t[:]))
        w1_dealt = w1_raw[:].rearrange("p j (m t) -> p t m j", t=PACK)
        w1_grouped = []
        for t in range(PACK):
            grouped = keep.tile([P, P, PACK], BF16, name="w1_grouped%d" % t, align_bytes=64)
            if t < 2:
                nc.vector.tensor_copy(grouped[:], w1_dealt[:, t])
            else:
                nc.scalar.copy(grouped[:], w1_dealt[:, t])
            w1_grouped.append(grouped)

        def quantise_w1(t):
            codes = keep.tile([P, P], U32, name="w1_codes%d" % t, align_bytes=64)
            scales = keep.tile([P, P], U8, name="w1_scales%d" % t, align_bytes=64)
            nc.vector.quantize_mx(out=codes[:].bitcast(FP8X4), scales=scales[:], in_=w1_grouped[t][:].rearrange("p m j -> p (m j)"))
            return codes, scales

        w1_mx = [quantise_w1(0)]
        x_code = keep.tile([P, S], U32, name="x_code", align_bytes=64)
        for h in range(HALVES):
            nc.vector.tensor_copy(x_code[:, h * HALF : (h + 1) * HALF], x_word_table[:].indirect(offs_t[:, h * HALF // 16 : (h + 1) * HALF // 16]))
        w1_mx.extend(quantise_w1(t) for t in range(1, PACK))

        half_y, r1, m1_windows, m1_plain = [], [], [], []
        y_plain = []
        for t in range(PACK):
            codes, scales = w1_mx[t]
            plain = keep.tile([P, S], F32, name="y_plain%d" % t)
            width = HALF if t == 0 else S
            for s0 in range(0, S, width):
                cols = slice(s0, s0 + width)
                acc = psum.tile([P, S], F32, name="acc", bufs=2)
                nc.tensor.matmul_mx(out=acc[:, :width], lhsT=codes[:].bitcast(FP8X4), lhsT_scale=scales[:], rhs=x_code[:, cols].bitcast(FP8X4), rhs_scale=x_scale[:, cols], start=True, stop=True)
                nc.scalar.activation(y_windows[t][:, cols], acc[:, :width], COPY, scale=gain[:, t : t + 1])
                if (t, s0) == (0, 0):
                    nc.vector.tensor_scalar(plain[:, cols], acc[:, :width], gain[:, t : t + 1], None, ALU.mult)
                else:
                    nc.scalar.activation(plain[:, cols], acc[:, :width], COPY, scale=gain[:, t : t + 1])
            y_plain.append(plain)

        for t in range(PACK):
            u = work.tile([P, S], F32, name="u1")
            width = HALF if t == 0 else S
            for s0 in range(0, S, width):
                cols = slice(s0, s0 + width)
                nc.vector.tensor_tensor(u[:, cols], y_windows[t][:].indirect(p1_t[:, s0 // 16 : (s0 + width) // 16]), y_plain[t][:, cols], ALU.subtract)
            v = work.tile([P, S], F32, name="v1")
            nc.vector.tensor_tensor(v[:], y_windows[t][:].indirect(p2_t[:]), y_plain[t][:], ALU.subtract)
            step = keep.tile([P, S], F32, name="r1_%d" % t)
            minmod(u, v, step[:], S)
            r1.append(step)
            turned = psum.tile([P, S // P, P], F32, name="turned", bufs=2)
            for c in range(S // P):
                cols = slice(c * P, (c + 1) * P)
                add_transposed(turned[:, c, :], [y_plain[t][:, cols], step[:, cols]])
            turned_sb = work.tile([P, S // P, P], F32, name="turned_sb")
            nc.scalar.copy(turned_sb[:], turned[:])
            back = psum.tile([P, S // P, P], F32, name="back", bufs=1)
            for c in range(S // P):
                add_transposed(back[:, c, :], [turned_sb[:, c, :]])
            window = keep.tile([P, S], F32, name="m1_window%d" % t)
            nc.scalar.copy(window[:], back[:].rearrange("p c s -> p (c s)"))
            plain = keep.tile([P, S], F32, name="m1_plain%d" % t)
            nc.scalar.copy(plain[:], back[:].rearrange("p c s -> p (c s)"))
            m1_windows.append(window)
            m1_plain.append(plain)

        for t in range(PACK):
            half = keep.tile([P, S], F32, name="half_y%d" % t)
            nc.scalar.activation(half[:], y_plain[t][:], COPY, scale=0.5)
            half_y.append(half)

        w2_grouped = keep.tile([P, PACK, P, PACK], BF16, name="w2_grouped", align_bytes=64)
        for t in range(PACK):
            nc.scalar.copy(w2_grouped[:, t], w2_raw[:].rearrange("p j (m t) -> p t m j", t=PACK)[:, t])
        w2_codes = keep.tile([P, N], U32, name="w2_codes", align_bytes=64)
        w2_scales = keep.tile([P, N], U8, name="w2_scales", align_bytes=64)
        nc.vector.quantize_mx(out=w2_codes[:].bitcast(FP8X4), scales=w2_scales[:], in_=w2_grouped[:].rearrange("p t m j -> p (t m j)"))

        z_mx = []
        for h in range(HALVES):
            entries = slice(h * HALF // 16, (h + 1) * HALF // 16)
            samples = slice(h * HALF, (h + 1) * HALF)
            z_turned = [psum.tile([P, PACK, P], F32, name="z_turned%d" % c, bufs=1) for c in range(CHUNKS)]
            for t0 in range(0, PACK, 2):
                u = work.tile([P, 2 * HALF], F32, name="u2")
                v = work.tile([P, 2 * HALF], F32, name="v2")
                for i in range(2):
                    part = slice(i * HALF, (i + 1) * HALF)
                    nc.vector.tensor_tensor(u[:, part], m1_windows[t0 + i][:].indirect(p3_t[:, entries]), m1_plain[t0 + i][:, samples], ALU.subtract)
                    nc.vector.tensor_tensor(v[:, part], m1_windows[t0 + i][:].indirect(p4_t[:, entries]), m1_plain[t0 + i][:, samples], ALU.subtract)
                r2 = work.tile([P, 2 * HALF], F32, name="r2")
                minmod(u, v, r2[:], 2 * HALF)
                for i in range(2):
                    t = t0 + i
                    for c in range(CHUNKS):
                        cols = slice(h * HALF + c * P, h * HALF + (c + 1) * P)
                        add_transposed(z_turned[c][:, t, :], [half_y[t][:, cols], r1[t][:, cols], r2[:, i * HALF + c * P : i * HALF + (c + 1) * P]])
            pairs = psum.tile([P, CHUNKS, 2, P], F32, name="pairs", bufs=1)
            for c in range(CHUNKS):
                z_rows = work.tile([P, 2, P, 2], BF16, name="z_rows")
                nc.scalar.activation(z_rows[:], z_turned[c][:].rearrange("s (u e) p -> s u p e", e=2), COPY, scale=-1.0)
                words = z_rows[:].rearrange("s u p e -> s (u p e)").bitcast(F32)
                for w in range(2):
                    nc.tensor.transpose(pairs[:, c, w, :], words[:, w * P : (w + 1) * P], ident[:])
            grouped = work.tile([P, HALF * PACK], BF16, name="z_grouped", align_bytes=64)
            nc.scalar.copy(
                grouped[:].bitcast(F32).rearrange("p (c s w) -> p c s w", c=CHUNKS, w=2),
                pairs[:].rearrange("p c w s -> p c s w"),
            )
            z_codes = work.tile([P, HALF], U32, name="z_codes", align_bytes=64)
            z_scales = work.tile([P, HALF], U8, name="z_scales", align_bytes=64)
            nc.vector.quantize_mx(out=z_codes[:].bitcast(FP8X4), scales=z_scales[:], in_=grouped[:])
            z_mx.append((z_codes, z_scales))

        def put_back(h, t, acc):
            z_codes, z_scales = z_mx[h]
            cols = slice(t * P, (t + 1) * P)
            nc.tensor.matmul_mx(out=acc[:, :HALF], lhsT=w2_codes[:, cols].bitcast(FP8X4), lhsT_scale=w2_scales[:, cols], rhs=z_codes[:].bitcast(FP8X4), rhs_scale=z_scales[:], start=True, stop=True)
            result = work.tile([P, HALF], F32, name="result", bufs=4)
            nc.scalar.copy(result[:], acc[:, :HALF])
            nc.vector.tensor_copy(pages[t][:].indirect(slot_t[:, h * HALF // 16 : (h + 1) * HALF // 16]), result[:])

        for h in range(HALVES):
            for t in range(PACK):
                if (h, t) == (0, PACK - 1):
                    put_back(h, t, psum.tile([P, S], F32, name="pairs", bufs=1))
                else:
                    put_back(h, t, psum.tile([P, S], F32, name="acc", bufs=2))

        for t in range(PACK):
            nc.sync.dma_start(out.rearrange("(p t) u -> t p u", t=PACK)[t], pages[t][:])
